import numpy as np
import ml_dtypes


def mxq(x, axis, fmt="e4m3"):
    dtype, down = {"e4m3": (ml_dtypes.float8_e4m3fn, 7), "e5m2": (ml_dtypes.float8_e5m2, 14)}[fmt]
    v = np.moveaxis(np.asarray(x, np.float32).astype(ml_dtypes.bfloat16).astype(np.float64), axis, -1)
    blocks = v.reshape(v.shape[:-1] + (-1, 32))
    amax = np.abs(blocks).max(-1, keepdims=True)
    byte = np.maximum(np.where(amax > 0, np.frexp(amax)[1] - 1 + 127, 0) - down, 1)
    scale = np.exp2(byte - 127.0)
    codes = (blocks / scale).astype(np.float32).astype(dtype).astype(np.float64)
    return np.moveaxis((codes * scale).reshape(v.shape), -1, axis)


WIDE = False


def mx_kscale(k):
    if not WIDE:
        return np.ones(k)
    levels = np.array([10, -10, 5, -5, 0])
    if k % 512:
        return np.exp2(np.random.permutation(np.resize(levels, k // 32))).repeat(32)
    a = np.empty((k // 512, 16))
    for p in range(k // 512):
        a[p, :8] = np.random.permutation(np.resize(levels, 8))
        for g in range(8):
            far = levels[np.abs(levels - a[p, g]) >= 10]
            a[p, g + 8] = far[np.random.randint(len(far))]
    return np.exp2(a.ravel()).repeat(32)


def f64(x):
    return np.asarray(x).astype(np.float64)


def striped(idx):
    return np.tile(idx.reshape(-1, 16).T, (8, 1)).astype(np.uint16)


def unstriped(offs):
    return offs[:16].T.reshape(-1).astype(np.int64)


def relu(v):
    return np.maximum(v, 0.0)


K, T, E, C, H, N = 1024, 1024, 8, 128, 512, 512


def by_expert(wq, xq):
    return np.concatenate([wq[e].T @ xq[:, e * C:(e + 1) * C] for e in range(E)], axis=1)


def setup_inputs():
    n = np.random.standard_normal
    s = mx_kscale(K)[:, None]
    u = mx_kscale(H)
    return {
        "xT": (n((K, T)) * s).astype(np.float32),
        "w1": (n((E, K, H)) / np.sqrt(K) / s[None] * u[None, None, :]).astype(np.float32),
        "w2": (n((E, H, N)) / np.sqrt(H) / u[None, :, None]).astype(np.float32),
        "gate": np.tile(np.random.uniform(0.2, 1.0, E * C), (N, 1)).astype(np.float32),
        "offs": striped(np.random.permutation(T)[:E * C]),
    }


def reference(xT, w1, w2, gate, offs):
    idx = unstriped(offs)
    xq = mxq(f64(xT)[:, idx], 0, "e4m3")
    h = relu(by_expert(mxq(f64(w1), 1, "e4m3"), xq))
    y = by_expert(mxq(f64(w2), 1, "e4m3"), mxq(h, 0, "e4m3"))
    out = np.zeros((N, T))
    out[:, idx] = f64(gate) * y
    return out

@@ -1,0 +1,253 @@
+from contextlib import ExitStack
+
+import concourse.mybir as mybir
+
+K, T, E, C, H, N = 1024, 1024, 8, 128, 512, 512
+FLOPS = 2 * E * C * (K * H + H * N)
+
+F32 = mybir.dt.float32
+BF16 = mybir.dt.bfloat16
+U32 = mybir.dt.uint32
+U16 = mybir.dt.uint16
+U8 = mybir.dt.uint8
+FP8X4 = mybir.dt.float8_e4m3fn_x4
+MULT = mybir.AluOpType.mult
+ADD = mybir.AluOpType.add
+RELU = mybir.ActivationFunctionType.Relu
+
+P = 128
+PASSES = K // 512
+STAGE_BUFS = 10
+HALF = 512
+
+X_ENGINE = {(0, 0): "VS", (0, 1): "GS", (1, 0): "GS", (1, 1): "GS"}
+W2_ENGINE = ["VSVS", "GGGG", "GGGG", "GGGG", "GGGG", "GGGG", "GGGG", "VSVS"]
+GROUPS = [(0,), (1,), (2,), (3,), (4,), (5,), (6,), (7,)]
+
+
+def cast(nc, engine, out, in_):
+    if engine == "V":
+        nc.vector.tensor_copy(out=out, in_=in_)
+    elif engine == "S":
+        nc.scalar.copy(out=out, in_=in_)
+    else:
+        nc.gpsimd.tensor_scalar(out, in_, 1.0, 0.0, op0=MULT, op1=ADD)
+
+
+def tile_routed_moe_kernel(tc, xT, w1, w2, gate, offs, out):
+    nc = tc.nc
+    with ExitStack() as ctx:
+        lists = ctx.enter_context(tc.tile_pool(name="lists", bufs=1))
+        keep = ctx.enter_context(tc.tile_pool(name="keep", bufs=1))
+        stage = ctx.enter_context(tc.tile_pool(name="stage", bufs=STAGE_BUFS))
+        grouped1 = ctx.enter_context(tc.tile_pool(name="grouped1", bufs=4))
+        grouped2 = ctx.enter_context(tc.tile_pool(name="grouped2", bufs=3))
+        codes1 = ctx.enter_context(tc.tile_pool(name="codes1", bufs=8))
+        codes2 = ctx.enter_context(tc.tile_pool(name="codes2", bufs=4))
+        small = ctx.enter_context(tc.tile_pool(name="small", bufs=3))
+        psum_a = ctx.enter_context(tc.psum_pool(name="psum_a", bufs=3))
+        psum_y = ctx.enter_context(tc.psum_pool(name="psum_y", bufs=4))
+
+        offs_sb = lists.tile([P, E * C // 16], U16, name="offs_sb")
+        nc.sync.dma_start(offs_sb[:], offs)
+
+        pairs = {}
+        for g in range(PASSES):
+            for u in range(2):
+                pairs[(g, u)] = keep.tile([P, T, 2], BF16, name="pairs%d%d" % (g, u), align_bytes=64)
+        xg = [keep.tile([P, E * C, 4], BF16, name="xg%d" % g, align_bytes=64) for g in range(PASSES)]
+        xc = [keep.tile([P, E * C], U32, name="xc%d" % g, align_bytes=64) for g in range(PASSES)]
+        xs = [keep.tile([P, E * C], U8, name="xs%d" % g, align_bytes=64) for g in range(PASSES)]
+        gate_sb = keep.tile([P, E * C], F32, name="gate_sb")
+        out_sb = [keep.tile([P, T], F32, name="out_sb%d" % b) for b in range(4)]
+
+        x_view = xT.rearrange("(g p u e) n -> g u p e n", g=PASSES, p=P, u=2, e=2)
+
+        units = [("x", g, u) for g in range(PASSES) for u in range(2)]
+        units += [("w1", 0, 0), ("w1", 0, 1), ("w2", 0, 0)]
+        for e in range(1, E - 1):
+            units += [("w2", e, 0), ("w1", e, 0), ("w1", e, 1)]
+        units += [("w1", E - 1, 0), ("w1", E - 1, 1), ("w2", E - 1, 0)]
+        raws = {}
+
+        def load(i):
+            kind, a, b = units[i]
+            if kind == "x":
+                raw = stage.tile([P, 2, T], F32, name="raw", tag="raw")
+                nc.sync.dma_start(out=raw[:], in_=x_view[a, b])
+            elif kind == "w1":
+                raw = stage.tile([P, 4, H], F32, name="raw", tag="raw")
+                nc.sync.dma_start(out=raw[:], in_=w1[a].rearrange("(g p j) i -> g p j i", g=PASSES, p=P, j=4)[b])
+            else:
+                raw = stage.tile([P, 4, N], F32, name="raw", tag="raw")
+                nc.sync.dma_start(out=raw[:], in_=w2[a].rearrange("(p j) n -> p j n", p=P, j=4))
+                if a == 0:
+                    nc.sync.dma_start(out=gate_sb[:], in_=gate[0:P, :])
+            raws[i] = raw
+
+        w1c = {}
+        w2c = {}
+        hc = {}
+        ysb = {}
+
+        def do_x(i, g, u):
+            raw = raws[i]
+            for s in range(2):
+                cast(
+                    nc,
+                    X_ENGINE[(g, u)][s],
+                    pairs[(g, u)][:, s * HALF : (s + 1) * HALF, :].rearrange("p (c i) e -> p c e i", i=4),
+                    raw[:, :, s * HALF : (s + 1) * HALF].rearrange("p e (c i) -> p c e i", i=4),
+                )
+            window = pairs[(g, u)][:].rearrange("p n e -> p (n e)").bitcast(U32)
+            words = xg[g][:].rearrange("p n t -> p (n t)").bitcast(U32).rearrange("p (n u) -> p n u", u=2)
+            for s in range(2):
+                nc.vector.tensor_copy(
+                    out=words[:, s * HALF : (s + 1) * HALF, u],
+                    in_=window.indirect(offs_sb[:, s * (HALF // 16) : (s + 1) * (HALF // 16)]),
+                )
+            if u == 1:
+                for s in range(2):
+                    cols = slice(s * HALF, (s + 1) * HALF)
+                    nc.vector.quantize_mx(
+                        out=xc[g][:, cols].bitcast(FP8X4),
+                        scales=xs[g][:, cols],
+                        in_=xg[g][:, cols, :].rearrange("p n t -> p (n t)"),
+                    )
+
+        def do_w1(i, e, g):
+            raw = raws[i]
+            wg = grouped1.tile([P, 4 * H], BF16, name="wg", tag="wg", align_bytes=64)
+            cast(
+                nc,
+                "S",
+                wg[:].rearrange("p (t m j) -> p m j t", t=4, m=P, j=4),
+                raw[:].rearrange("p j (m t) -> p m j t", t=4),
+            )
+            wc = codes1.tile([P, H], U32, name="wc", tag="wc", align_bytes=64)
+            ws = codes1.tile([P, H], U8, name="ws", tag="ws", align_bytes=64)
+            nc.vector.quantize_mx(out=wc[:].bitcast(FP8X4), scales=ws[:], in_=wg[:])
+            w1c[(e, g)] = (wc, ws)
+
+
+        def layer1(e):
+            a_ps = psum_a.tile([P, 4, C], F32, name="a_ps", tag="a_ps")
+            slots = slice(e * C, (e + 1) * C)
+            for t in range(4):
+                for g in range(PASSES):
+                    wc, ws = w1c[(e, g)]
+                    nc.tensor.matmul_mx(
+                        out=a_ps[:, t, :],
+                        lhsT=wc[:, t * P : (t + 1) * P].bitcast(FP8X4),
+                        lhsT_scale=ws[:, t * P : (t + 1) * P],
+                        rhs=xc[g][:, slots].bitcast(FP8X4),
+                        rhs_scale=xs[g][:, slots],
+                        start=(g == 0),
+                        stop=(g == PASSES - 1),
+                    )
+            hb = small.tile([P, C, 4], BF16, name="hb", tag="hb", align_bytes=64)
+            nc.scalar.activation(out=hb[:], in_=a_ps[:].rearrange("p t n -> p n t"), func=RELU)
+            hcod = small.tile([P, C], U32, name="hcod", tag="hcod", align_bytes=64)
+            hsc = small.tile([P, C], U8, name="hsc", tag="hsc", align_bytes=64)
+            nc.vector.quantize_mx(out=hcod[:].bitcast(FP8X4), scales=hsc[:], in_=hb[:].rearrange("p n t -> p (n t)"))
+            hc[e] = (hcod, hsc)
+
+        def group_of(e):
+            for grp in GROUPS:
+                if e in grp:
+                    return grp
+            return None
+
+        def do_w2(i, e):
+            raw = raws[i]
+            wg = grouped2.tile([P, 4 * N], BF16, name="wg", tag="wg", align_bytes=64)
+            wc = codes2.tile([P, N], U32, name="wc", tag="wc", align_bytes=64)
+            ws = codes2.tile([P, N], U8, name="ws", tag="ws", align_bytes=64)
+            for b in range(4):
+                cast(
+                    nc,
+                    W2_ENGINE[e][b],
+                    wg[:, b * 4 * P : (b + 1) * 4 * P].rearrange("p (c i j) -> p c j i", i=4, j=4),
+                    raw[:, :, b * P : (b + 1) * P].rearrange("p j (c i) -> p c j i", i=4),
+                )
+            if e < E - 1:
+                nc.vector.quantize_mx(out=wc[:].bitcast(FP8X4), scales=ws[:], in_=wg[:])
+            else:
+                for b in range(4):
+                    cols = slice(b * P, (b + 1) * P)
+                    nc.vector.quantize_mx(
+                        out=wc[:, cols].bitcast(FP8X4), scales=ws[:, cols], in_=wg[:, b * 4 * P : (b + 1) * 4 * P]
+                    )
+            w2c[e] = (wc, ws)
+
+        def finish(e):
+            grp = group_of(e)
+            hcod, hsc = hc[e]
+            wc, ws = w2c[e]
+            if e < E - 1:
+                y_ps = psum_y.tile([P, 4, C], F32, name="y_ps", tag="y_ps")
+                for b in range(4):
+                    nc.tensor.matmul_mx(
+                        out=y_ps[:, b, :],
+                        lhsT=wc[:, b * P : (b + 1) * P].bitcast(FP8X4),
+                        lhsT_scale=ws[:, b * P : (b + 1) * P],
+                        rhs=hcod[:].bitcast(FP8X4),
+                        rhs_scale=hsc[:],
+                        start=True,
+                        stop=True,
+                    )
+                if e == grp[0]:
+                    ysb[grp] = small.tile([P, 4, C * len(grp)], F32, name="ysb", tag="ysb")
+                pos = grp.index(e)
+                gcols = slice(e * C, (e + 1) * C)
+                nc.vector.tensor_tensor(
+                    out=ysb[grp][:, :, pos * C : (pos + 1) * C],
+                    in0=y_ps[:],
+                    in1=gate_sb[:, gcols].unsqueeze(1).to_broadcast([P, 4, C]),
+                    op=MULT,
+                )
+                if e == grp[-1]:
+                    ocols = offs_sb[:, grp[0] * (C // 16) : (grp[-1] + 1) * (C // 16)]
+                    for b in range(4):
+                        nc.vector.tensor_copy(out=out_sb[b][:].indirect(ocols), in_=ysb[grp][:, b, :])
+            else:
+                ocols = offs_sb[:, e * (C // 16) : (e + 1) * (C // 16)]
+                gcols = slice(e * C, (e + 1) * C)
+                for b in range(4):
+                    cols = slice(b * P, (b + 1) * P)
+                    y_b = psum_y.tile([P, C], F32, name="y_ps", tag="y_ps")
+                    nc.tensor.matmul_mx(
+                        out=y_b[:],
+                        lhsT=wc[:, cols].bitcast(FP8X4),
+                        lhsT_scale=ws[:, cols],
+                        rhs=hcod[:].bitcast(FP8X4),
+                        rhs_scale=hsc[:],
+                        start=True,
+                        stop=True,
+                    )
+                    y_last = small.tile([P, C], F32, name="y_last", tag="y_last")
+                    nc.vector.tensor_tensor(out=y_last[:], in0=y_b[:], in1=gate_sb[:, gcols], op=MULT)
+                    nc.vector.tensor_copy(out=out_sb[b][:].indirect(ocols), in_=y_last[:])
+                    nc.sync.dma_start(out=out[b * P : (b + 1) * P, :], in_=out_sb[b][:])
+
+        for i in range(min(STAGE_BUFS, len(units))):
+            load(i)
+        done = {"x": 0, "l1": 0, "l2": 0}
+        for i in range(len(units)):
+            kind, a, b = units[i]
+            if kind == "x":
+                do_x(i, a, b)
+                done["x"] = done["x"] + 1
+            elif kind == "w1":
+                do_w1(i, a, b)
+            else:
+                do_w2(i, a)
+            if i + STAGE_BUFS < len(units):
+                load(i + STAGE_BUFS)
+            if done["x"] == 2 * PASSES:
+                while done["l1"] < E and (done["l1"], PASSES - 1) in w1c:
+                    layer1(done["l1"])
+                    done["l1"] = done["l1"] + 1
+                while done["l2"] < done["l1"] and done["l2"] in w2c:
+                    finish(done["l2"])
+                    done["l2"] = done["l2"] + 1

@@ -200,16 +200,14 @@ def tile_routed_moe_kernel(tc, xT, w1, w2, gate, offs, out):
                     ysb[grp] = small.tile([P, 4, C * len(grp)], F32, name="ysb", tag="ysb")
                 pos = grp.index(e)
                 gcols = slice(e * C, (e + 1) * C)
-                nc.vector.tensor_tensor(
-                    out=ysb[grp][:, :, pos * C : (pos + 1) * C],
-                    in0=y_ps[:],
-                    in1=gate_sb[:, gcols].unsqueeze(1).to_broadcast([P, 4, C]),
-                    op=MULT,
-                )
+                nc.scalar.copy(out=ysb[grp][:, :, pos * C : (pos + 1) * C], in_=y_ps[:])
                 if e == grp[-1]:
                     ocols = offs_sb[:, grp[0] * (C // 16) : (grp[-1] + 1) * (C // 16)]
+                    gall = slice(grp[0] * C, (grp[-1] + 1) * C)
                     for b in range(4):
-                        nc.vector.tensor_copy(out=out_sb[b][:].indirect(ocols), in_=ysb[grp][:, b, :])
+                        nc.vector.tensor_tensor(
+                            out=out_sb[b][:].indirect(ocols), in0=ysb[grp][:, b, :], in1=gate_sb[:, gall], op=MULT
+                        )
             else:
                 ocols = offs_sb[:, e * (C // 16) : (e + 1) * (C // 16)]
                 gcols = slice(e * C, (e + 1) * C)

@@ -64,10 +64,10 @@ def tile_routed_moe_kernel(tc, xT, w1, w2, gate, offs, out):
         x_view = xT.rearrange("(g p u e) n -> g u p e n", g=PASSES, p=P, u=2, e=2)
 
         units = [("x", g, u) for g in range(PASSES) for u in range(2)]
-        units += [("w1", 0, 0), ("w1", 0, 1), ("w2", 0, 0)]
-        for e in range(1, E - 1):
-            units += [("w2", e, 0), ("w1", e, 0), ("w1", e, 1)]
-        units += [("w1", E - 1, 0), ("w1", E - 1, 1), ("w2", E - 1, 0)]
+        units += [("w1", 0, 0)]
+        for e in range(E - 1):
+            units += [("w1", e, 1), ("w1", e + 1, 0), ("w2", e, 0)]
+        units += [("w1", E - 1, 1), ("w2", E - 1, 0)]
         raws = {}
 
         def load(i):

@@ -21,7 +21,7 @@ STAGE_BUFS = 10
 HALF = 512
 
 X_ENGINE = {(0, 0): "VS", (0, 1): "GS", (1, 0): "GS", (1, 1): "GS"}
-W2_ENGINE = ["VSVS", "GGGG", "GGGG", "GGGG", "GGGG", "GGGG", "GGGG", "VSVS"]
+W2_ENGINE = ["VSVS", "GSGS", "GSGS", "GSGS", "GSGS", "GSGS", "GSGS", "VSVS"]
 GROUPS = [(0,), (1,), (2,), (3,), (4,), (5,), (6,), (7,)]
 
 

@@ -21,7 +21,7 @@ STAGE_BUFS = 10
 HALF = 512
 
 X_ENGINE = {(0, 0): "VS", (0, 1): "GS", (1, 0): "GS", (1, 1): "GS"}
-W2_ENGINE = ["VSVS", "GSGS", "GSGS", "GSGS", "GSGS", "GSGS", "GSGS", "VSVS"]
+W2_ENGINE = ["GSGS", "GSGS", "GSGS", "GSGS", "GSGS", "GSGS", "GSGS", "GSGS"]
 GROUPS = [(0,), (1,), (2,), (3,), (4,), (5,), (6,), (7,)]
 
 
@@ -75,14 +75,14 @@ def tile_routed_moe_kernel(tc, xT, w1, w2, gate, offs, out):
             if kind == "x":
                 raw = stage.tile([P, 2, T], F32, name="raw", tag="raw")
                 nc.sync.dma_start(out=raw[:], in_=x_view[a, b])
+                if (a, b) == (PASSES - 1, 1):
+                    nc.sync.dma_start(out=gate_sb[:], in_=gate[0:P, :])
             elif kind == "w1":
                 raw = stage.tile([P, 4, H], F32, name="raw", tag="raw")
                 nc.sync.dma_start(out=raw[:], in_=w1[a].rearrange("(g p j) i -> g p j i", g=PASSES, p=P, j=4)[b])
             else:
                 raw = stage.tile([P, 4, N], F32, name="raw", tag="raw")
                 nc.sync.dma_start(out=raw[:], in_=w2[a].rearrange("(p j) n -> p j n", p=P, j=4))
-                if a == 0:
-                    nc.sync.dma_start(out=gate_sb[:], in_=gate[0:P, :])
             raws[i] = raw
 
         w1c = {}

@@ -19,10 +19,10 @@ P = 128
 PASSES = K // 512
 STAGE_BUFS = 10
 HALF = 512
+TAIL = 2 * C
 
 X_ENGINE = {(0, 0): "VS", (0, 1): "GS", (1, 0): "GS", (1, 1): "GS"}
-W2_ENGINE = ["GSGS", "GSGS", "GSGS", "GSGS", "GSGS", "GSGS", "GSGS", "GSGS"]
-GROUPS = [(0,), (1,), (2,), (3,), (4,), (5,), (6,), (7,)]
+W2_ENGINE = "VSVS"
 
 
 def cast(nc, engine, out, in_):
@@ -32,6 +32,14 @@ def cast(nc, engine, out, in_):
         nc.scalar.copy(out=out, in_=in_)
     else:
         nc.gpsimd.tensor_scalar(out, in_, 1.0, 0.0, op0=MULT, op1=ADD)
+
+
+def gate_slots(kind, e, g):
+    if kind == "w1" and g == 0 and e >= 2:
+        return e - 2, e - 1
+    if kind == "w2" and e == E - 1:
+        return E - 2, E
+    return None
 
 
 def tile_routed_moe_kernel(tc, xT, w1, w2, gate, offs, out):
@@ -58,10 +66,11 @@ def tile_routed_moe_kernel(tc, xT, w1, w2, gate, offs, out):
         xg = [keep.tile([P, E * C, 4], BF16, name="xg%d" % g, align_bytes=64) for g in range(PASSES)]
         xc = [keep.tile([P, E * C], U32, name="xc%d" % g, align_bytes=64) for g in range(PASSES)]
         xs = [keep.tile([P, E * C], U8, name="xs%d" % g, align_bytes=64) for g in range(PASSES)]
-        gate_sb = keep.tile([P, E * C], F32, name="gate_sb")
         out_sb = [keep.tile([P, T], F32, name="out_sb%d" % b) for b in range(4)]
 
         x_view = xT.rearrange("(g p u e) n -> g u p e n", g=PASSES, p=P, u=2, e=2)
+        w1_view = w1.rearrange("e (g p j) i -> e g p j i", g=PASSES, p=P, j=4)
+        w2_view = w2.rearrange("e (p j) n -> e p j n", p=P, j=4)
 
         units = [("x", g, u) for g in range(PASSES) for u in range(2)]
         units += [("w1", 0, 0)]
@@ -69,26 +78,31 @@ def tile_routed_moe_kernel(tc, xT, w1, w2, gate, offs, out):
             units += [("w1", e, 1), ("w1", e + 1, 0), ("w2", e, 0)]
         units += [("w1", E - 1, 1), ("w2", E - 1, 0)]
         raws = {}
+        gates = {}
 
         def load(i):
             kind, a, b = units[i]
+            raw = stage.tile([P, 4 * H + TAIL], F32, name="raw", tag="raw")
             if kind == "x":
-                raw = stage.tile([P, 2, T], F32, name="raw", tag="raw")
-                nc.sync.dma_start(out=raw[:], in_=x_view[a, b])
-                if (a, b) == (PASSES - 1, 1):
-                    nc.sync.dma_start(out=gate_sb[:], in_=gate[0:P, :])
+                view = raw[:, : 2 * T].rearrange("p (e n) -> p e n", e=2)
+                nc.sync.dma_start(out=view, in_=x_view[a, b])
             elif kind == "w1":
-                raw = stage.tile([P, 4, H], F32, name="raw", tag="raw")
-                nc.sync.dma_start(out=raw[:], in_=w1[a].rearrange("(g p j) i -> g p j i", g=PASSES, p=P, j=4)[b])
+                view = raw[:, : 4 * H].rearrange("p (j i) -> p j i", j=4)
+                nc.sync.dma_start(out=view, in_=w1_view[a, b])
             else:
-                raw = stage.tile([P, 4, N], F32, name="raw", tag="raw")
-                nc.sync.dma_start(out=raw[:], in_=w2[a].rearrange("(p j) n -> p j n", p=P, j=4))
-            raws[i] = raw
+                view = raw[:, : 4 * N].rearrange("p (j n) -> p j n", j=4)
+                nc.sync.dma_start(out=view, in_=w2_view[a])
+            raws[i] = view
+            slots = gate_slots(kind, a, b)
+            if slots is not None:
+                lo, hi = slots
+                nc.sync.dma_start(out=raw[:, 4 * H : 4 * H + (hi - lo) * C], in_=gate[0:P, lo * C : hi * C])
+                for e in range(lo, hi):
+                    gates[e] = raw[:, 4 * H + (e - lo) * C : 4 * H + (e - lo + 1) * C]
 
         w1c = {}
         w2c = {}
         hc = {}
-        ysb = {}
 
         def do_x(i, g, u):
             raw = raws[i]
@@ -116,19 +130,17 @@ def tile_routed_moe_kernel(tc, xT, w1, w2, gate, offs, out):
                     )
 
         def do_w1(i, e, g):
-            raw = raws[i]
             wg = grouped1.tile([P, 4 * H], BF16, name="wg", tag="wg", align_bytes=64)
             cast(
                 nc,
                 "S",
                 wg[:].rearrange("p (t m j) -> p m j t", t=4, m=P, j=4),
-                raw[:].rearrange("p j (m t) -> p m j t", t=4),
+                raws[i].rearrange("p j (m t) -> p m j t", t=4),
             )
             wc = codes1.tile([P, H], U32, name="wc", tag="wc", align_bytes=64)
             ws = codes1.tile([P, H], U8, name="ws", tag="ws", align_bytes=64)
             nc.vector.quantize_mx(out=wc[:].bitcast(FP8X4), scales=ws[:], in_=wg[:])
             w1c[(e, g)] = (wc, ws)
-
 
         def layer1(e):
             a_ps = psum_a.tile([P, 4, C], F32, name="a_ps", tag="a_ps")
@@ -152,12 +164,6 @@ def tile_routed_moe_kernel(tc, xT, w1, w2, gate, offs, out):
             nc.vector.quantize_mx(out=hcod[:].bitcast(FP8X4), scales=hsc[:], in_=hb[:].rearrange("p n t -> p (n t)"))
             hc[e] = (hcod, hsc)
 
-        def group_of(e):
-            for grp in GROUPS:
-                if e in grp:
-                    return grp
-            return None
-
         def do_w2(i, e):
             raw = raws[i]
             wg = grouped2.tile([P, 4 * N], BF16, name="wg", tag="wg", align_bytes=64)
@@ -166,66 +172,38 @@ def tile_routed_moe_kernel(tc, xT, w1, w2, gate, offs, out):
             for b in range(4):
                 cast(
                     nc,
-                    W2_ENGINE[e][b],
+                    W2_ENGINE[b],
                     wg[:, b * 4 * P : (b + 1) * 4 * P].rearrange("p (c i j) -> p c j i", i=4, j=4),
                     raw[:, :, b * P : (b + 1) * P].rearrange("p j (c i) -> p c j i", i=4),
                 )
-            if e < E - 1:
-                nc.vector.quantize_mx(out=wc[:].bitcast(FP8X4), scales=ws[:], in_=wg[:])
-            else:
-                for b in range(4):
-                    cols = slice(b * P, (b + 1) * P)
-                    nc.vector.quantize_mx(
-                        out=wc[:, cols].bitcast(FP8X4), scales=ws[:, cols], in_=wg[:, b * 4 * P : (b + 1) * 4 * P]
-                    )
+            step = 4 if e < E - 1 else 1
+            for b in range(0, 4, step):
+                cols = slice(b * P, (b + step) * P)
+                nc.vector.quantize_mx(
+                    out=wc[:, cols].bitcast(FP8X4), scales=ws[:, cols], in_=wg[:, b * 4 * P : (b + step) * 4 * P]
+                )
             w2c[e] = (wc, ws)
 
         def finish(e):
-            grp = group_of(e)
             hcod, hsc = hc[e]
             wc, ws = w2c[e]
-            if e < E - 1:
-                y_ps = psum_y.tile([P, 4, C], F32, name="y_ps", tag="y_ps")
-                for b in range(4):
-                    nc.tensor.matmul_mx(
-                        out=y_ps[:, b, :],
-                        lhsT=wc[:, b * P : (b + 1) * P].bitcast(FP8X4),
-                        lhsT_scale=ws[:, b * P : (b + 1) * P],
-                        rhs=hcod[:].bitcast(FP8X4),
-                        rhs_scale=hsc[:],
-                        start=True,
-                        stop=True,
-                    )
-                if e == grp[0]:
-                    ysb[grp] = small.tile([P, 4, C * len(grp)], F32, name="ysb", tag="ysb")
-                pos = grp.index(e)
-                gcols = slice(e * C, (e + 1) * C)
-                nc.scalar.copy(out=ysb[grp][:, :, pos * C : (pos + 1) * C], in_=y_ps[:])
-                if e == grp[-1]:
-                    ocols = offs_sb[:, grp[0] * (C // 16) : (grp[-1] + 1) * (C // 16)]
-                    gall = slice(grp[0] * C, (grp[-1] + 1) * C)
-                    for b in range(4):
-                        nc.vector.tensor_tensor(
-                            out=out_sb[b][:].indirect(ocols), in0=ysb[grp][:, b, :], in1=gate_sb[:, gall], op=MULT
-                        )
-            else:
-                ocols = offs_sb[:, e * (C // 16) : (e + 1) * (C // 16)]
-                gcols = slice(e * C, (e + 1) * C)
-                for b in range(4):
-                    cols = slice(b * P, (b + 1) * P)
-                    y_b = psum_y.tile([P, C], F32, name="y_ps", tag="y_ps")
-                    nc.tensor.matmul_mx(
-                        out=y_b[:],
-                        lhsT=wc[:, cols].bitcast(FP8X4),
-                        lhsT_scale=ws[:, cols],
-                        rhs=hcod[:].bitcast(FP8X4),
-                        rhs_scale=hsc[:],
-                        start=True,
-                        stop=True,
-                    )
-                    y_last = small.tile([P, C], F32, name="y_last", tag="y_last")
-                    nc.vector.tensor_tensor(out=y_last[:], in0=y_b[:], in1=gate_sb[:, gcols], op=MULT)
-                    nc.vector.tensor_copy(out=out_sb[b][:].indirect(ocols), in_=y_last[:])
+            ocols = offs_sb[:, e * (C // 16) : (e + 1) * (C // 16)]
+            for b in range(4):
+                cols = slice(b * P, (b + 1) * P)
+                y_ps = psum_y.tile([P, C], F32, name="y_ps", tag="y_ps")
+                nc.tensor.matmul_mx(
+                    out=y_ps[:],
+                    lhsT=wc[:, cols].bitcast(FP8X4),
+                    lhsT_scale=ws[:, cols],
+                    rhs=hcod[:].bitcast(FP8X4),
+                    rhs_scale=hsc[:],
+                    start=True,
+                    stop=True,
+                )
+                y_sb = small.tile([P, C], F32, name="y_sb", tag="y_sb", bufs=8)
+                nc.vector.tensor_tensor(out=y_sb[:], in0=y_ps[:], in1=gates[e], op=MULT)
+                nc.vector.tensor_copy(out=out_sb[b][:].indirect(ocols), in_=y_sb[:])
+                if e == E - 1:
                     nc.sync.dma_start(out=out[b * P : (b + 1) * P, :], in_=out_sb[b][:])
 
         for i in range(min(STAGE_BUFS, len(units))):
@@ -246,6 +224,6 @@ def tile_routed_moe_kernel(tc, xT, w1, w2, gate, offs, out):
                 while done["l1"] < E and (done["l1"], PASSES - 1) in w1c:
                     layer1(done["l1"])
                     done["l1"] = done["l1"] + 1
-                while done["l2"] < done["l1"] and done["l2"] in w2c:
+                while done["l2"] < done["l1"] and done["l2"] in w2c and done["l2"] in gates:
                     finish(done["l2"])
                     done["l2"] = done["l2"] + 1

@@ -22,7 +22,7 @@ HALF = 512
 TAIL = 2 * C
 
 X_ENGINE = {(0, 0): "VS", (0, 1): "GS", (1, 0): "GS", (1, 1): "GS"}
-W2_ENGINE = "VSVS"
+W2_ENGINE = "GSGS"
 
 
 def cast(nc, engine, out, in_):
@@ -73,8 +73,8 @@ def tile_routed_moe_kernel(tc, xT, w1, w2, gate, offs, out):
         w2_view = w2.rearrange("e (p j) n -> e p j n", p=P, j=4)
 
         units = [("x", g, u) for g in range(PASSES) for u in range(2)]
-        units += [("w1", 0, 0)]
-        for e in range(E - 1):
+        units += [("w1", 0, 0), ("w1", 1, 0), ("w2", 0, 0), ("w1", 0, 1)]
+        for e in range(1, E - 1):
             units += [("w1", e, 1), ("w1", e + 1, 0), ("w2", e, 0)]
         units += [("w1", E - 1, 1), ("w2", E - 1, 0)]
         raws = {}

@@ -22,7 +22,7 @@ HALF = 512
 TAIL = 2 * C
 
 X_ENGINE = {(0, 0): "VS", (0, 1): "GS", (1, 0): "GS", (1, 1): "GS"}
-W2_ENGINE = "GSGS"
+W2_ENGINE = ["GSGS"] * (E - 1) + ["SSSS"]
 
 
 def cast(nc, engine, out, in_):
@@ -172,7 +172,7 @@ def tile_routed_moe_kernel(tc, xT, w1, w2, gate, offs, out):
             for b in range(4):
                 cast(
                     nc,
-                    W2_ENGINE[b],
+                    W2_ENGINE[e][b],
                     wg[:, b * 4 * P : (b + 1) * 4 * P].rearrange("p (c i j) -> p c j i", i=4, j=4),
                     raw[:, :, b * P : (b + 1) * P].rearrange("p j (c i) -> p c j i", i=4),
                 )
@@ -188,23 +188,32 @@ def tile_routed_moe_kernel(tc, xT, w1, w2, gate, offs, out):
             hcod, hsc = hc[e]
             wc, ws = w2c[e]
             ocols = offs_sb[:, e * (C // 16) : (e + 1) * (C // 16)]
-            for b in range(4):
-                cols = slice(b * P, (b + 1) * P)
-                y_ps = psum_y.tile([P, C], F32, name="y_ps", tag="y_ps")
-                nc.tensor.matmul_mx(
-                    out=y_ps[:],
-                    lhsT=wc[:, cols].bitcast(FP8X4),
-                    lhsT_scale=ws[:, cols],
-                    rhs=hcod[:].bitcast(FP8X4),
-                    rhs_scale=hsc[:],
-                    start=True,
-                    stop=True,
+            width = 2 if e < E - 1 else 1
+            for b0 in range(0, 4, width):
+                y_ps = psum_y.tile([P, width, C], F32, name="y_ps", tag="y_ps")
+                for r in range(width):
+                    cols = slice((b0 + r) * P, (b0 + r + 1) * P)
+                    nc.tensor.matmul_mx(
+                        out=y_ps[:, r, :],
+                        lhsT=wc[:, cols].bitcast(FP8X4),
+                        lhsT_scale=ws[:, cols],
+                        rhs=hcod[:].bitcast(FP8X4),
+                        rhs_scale=hsc[:],
+                        start=True,
+                        stop=True,
+                    )
+                y_sb = small.tile([P, width, C], F32, name="y_sb", tag="y_sb%d" % width, bufs=8 // width)
+                nc.vector.tensor_tensor(
+                    out=y_sb[:],
+                    in0=y_ps[:],
+                    in1=gates[e].unsqueeze(1).to_broadcast([P, width, C]),
+                    op=MULT,
                 )
-                y_sb = small.tile([P, C], F32, name="y_sb", tag="y_sb", bufs=8)
-                nc.vector.tensor_tensor(out=y_sb[:], in0=y_ps[:], in1=gates[e], op=MULT)
-                nc.vector.tensor_copy(out=out_sb[b][:].indirect(ocols), in_=y_sb[:])
-                if e == E - 1:
-                    nc.sync.dma_start(out=out[b * P : (b + 1) * P, :], in_=out_sb[b][:])
+                for r in range(width):
+                    b = b0 + r
+                    nc.vector.tensor_copy(out=out_sb[b][:].indirect(ocols), in_=y_sb[:, r, :])
+                    if e == E - 1:
+                        nc.sync.dma_start(out=out[b * P : (b + 1) * P, :], in_=out_sb[b][:])
 
         for i in range(min(STAGE_BUFS, len(units))):
             load(i)

@@ -157,7 +157,10 @@ def tile_routed_moe_kernel(tc, xT, w1, w2, gate, offs, out):
                         start=(g == 0),
                         stop=(g == PASSES - 1),
                     )
-            hb = small.tile([P, C, 4], BF16, name="hb", tag="hb", align_bytes=64)
+            if e == E - 1:
+                hb = small.tile([P, C, 4], BF16, name="hb", tag="tail_h", bufs=1, align_bytes=64)
+            else:
+                hb = small.tile([P, C, 4], BF16, name="hb", tag="hb", align_bytes=64)
             nc.scalar.activation(out=hb[:], in_=a_ps[:].rearrange("p t n -> p n t"), func=RELU)
             hcod = small.tile([P, C], U32, name="hcod", tag="hcod", align_bytes=64)
             hsc = small.tile([P, C], U8, name="hsc", tag="hsc", align_bytes=64)
@@ -184,36 +187,51 @@ def tile_routed_moe_kernel(tc, xT, w1, w2, gate, offs, out):
                 )
             w2c[e] = (wc, ws)
 
-        def finish(e):
+        def finish(e, b0, width, tag, bufs):
             hcod, hsc = hc[e]
             wc, ws = w2c[e]
             ocols = offs_sb[:, e * (C // 16) : (e + 1) * (C // 16)]
-            width = 2 if e < E - 1 else 1
-            for b0 in range(0, 4, width):
-                y_ps = psum_y.tile([P, width, C], F32, name="y_ps", tag="y_ps")
-                for r in range(width):
-                    cols = slice((b0 + r) * P, (b0 + r + 1) * P)
-                    nc.tensor.matmul_mx(
-                        out=y_ps[:, r, :],
-                        lhsT=wc[:, cols].bitcast(FP8X4),
-                        lhsT_scale=ws[:, cols],
-                        rhs=hcod[:].bitcast(FP8X4),
-                        rhs_scale=hsc[:],
-                        start=True,
-                        stop=True,
-                    )
-                y_sb = small.tile([P, width, C], F32, name="y_sb", tag="y_sb%d" % width, bufs=8 // width)
+            y_ps = psum_y.tile([P, width, C], F32, name="y_ps", tag="y_ps")
+            for r in range(width):
+                cols = slice((b0 + r) * P, (b0 + r + 1) * P)
+                nc.tensor.matmul_mx(
+                    out=y_ps[:, r, :],
+                    lhsT=wc[:, cols].bitcast(FP8X4),
+                    lhsT_scale=ws[:, cols],
+                    rhs=hcod[:].bitcast(FP8X4),
+                    rhs_scale=hsc[:],
+                    start=True,
+                    stop=True,
+                )
+            y_sb = small.tile([P, width, C], F32, name="y_sb", tag=tag, bufs=bufs, align_bytes=64)
+            if e < E - 1:
                 nc.vector.tensor_tensor(
                     out=y_sb[:],
                     in0=y_ps[:],
                     in1=gates[e].unsqueeze(1).to_broadcast([P, width, C]),
                     op=MULT,
                 )
-                for r in range(width):
-                    b = b0 + r
-                    nc.vector.tensor_copy(out=out_sb[b][:].indirect(ocols), in_=y_sb[:, r, :])
-                    if e == E - 1:
-                        nc.sync.dma_start(out=out[b * P : (b + 1) * P, :], in_=out_sb[b][:])
+            else:
+                nc.scalar.copy(out=y_sb[:], in_=y_ps[:])
+            for r in range(width):
+                window = out_sb[b0 + r][:].indirect(ocols)
+                if e < E - 1:
+                    nc.vector.tensor_copy(out=window, in_=y_sb[:, r, :])
+                else:
+                    nc.vector.tensor_tensor(out=window, in0=y_sb[:, r, :], in1=gates[e], op=MULT)
+
+        def store(b):
+            nc.sync.dma_start(out=out[b * P : (b + 1) * P, :], in_=out_sb[b][:])
+
+        def finish_last_two():
+            finish(E - 2, 0, 2, "y2", 4)
+            finish(E - 2, 2, 1, "tail_h", 1)
+            finish(E - 1, 0, 1, "tail_y", 1)
+            store(0)
+            finish(E - 2, 3, 1, "tail_y", 1)
+            for b in range(1, 4):
+                finish(E - 1, b, 1, "y1", 4)
+                store(b)
 
         for i in range(min(STAGE_BUFS, len(units))):
             load(i)
@@ -234,5 +252,10 @@ def tile_routed_moe_kernel(tc, xT, w1, w2, gate, offs, out):
                     layer1(done["l1"])
                     done["l1"] = done["l1"] + 1
                 while done["l2"] < done["l1"] and done["l2"] in w2c and done["l2"] in gates:
-                    finish(done["l2"])
-                    done["l2"] = done["l2"] + 1
+                    e = done["l2"]
+                    if e < E - 2:
+                        finish(e, 0, 2, "y2", 4)
+                        finish(e, 2, 2, "y2", 4)
+                    elif e == E - 1:
+                        finish_last_two()
+                    done["l2"] = e + 1

@@ -19,9 +19,8 @@ P = 128
 PASSES = K // 512
 STAGE_BUFS = 10
 HALF = 512
-TAIL = 2 * C
 
-X_ENGINE = {(0, 0): "VS", (0, 1): "GS", (1, 0): "GS", (1, 1): "GS"}
+X_ENGINE = {(0, 0): "VS", (0, 1): "S", (1, 0): "S", (1, 1): "S"}
 W2_ENGINE = ["GSGS"] * (E - 1) + ["SSSS"]
 
 
@@ -32,14 +31,6 @@ def cast(nc, engine, out, in_):
         nc.scalar.copy(out=out, in_=in_)
     else:
         nc.gpsimd.tensor_scalar(out, in_, 1.0, 0.0, op0=MULT, op1=ADD)
-
-
-def gate_slots(kind, e, g):
-    if kind == "w1" and g == 0 and e >= 2:
-        return e - 2, e - 1
-    if kind == "w2" and e == E - 1:
-        return E - 2, E
-    return None
 
 
 def tile_routed_moe_kernel(tc, xT, w1, w2, gate, offs, out):
@@ -62,9 +53,10 @@ def tile_routed_moe_kernel(tc, xT, w1, w2, gate, offs, out):
         pairs = {}
         for g in range(PASSES):
             for u in range(2):
-                pairs[(g, u)] = keep.tile([P, T, 2], BF16, name="pairs%d%d" % (g, u), align_bytes=64)
+                pairs[(g, u)] = keep.tile([P, T, 2], BF16, name="pairs%d%d" % (g, u), tag="pairs%d%d" % (g, u), align_bytes=64)
         xg = [keep.tile([P, E * C, 4], BF16, name="xg%d" % g, align_bytes=64) for g in range(PASSES)]
-        xc = [keep.tile([P, E * C], U32, name="xc%d" % g, align_bytes=64) for g in range(PASSES)]
+        picked = [keep.tile([P, 2, E * C, 2], BF16, name="picked%d" % g, align_bytes=64) for g in range(PASSES)]
+        xc = []
         xs = [keep.tile([P, E * C], U8, name="xs%d" % g, align_bytes=64) for g in range(PASSES)]
         out_sb = [keep.tile([P, T], F32, name="out_sb%d" % b) for b in range(4)]
 
@@ -78,11 +70,14 @@ def tile_routed_moe_kernel(tc, xT, w1, w2, gate, offs, out):
             units += [("w1", e, 1), ("w1", e + 1, 0), ("w2", e, 0)]
         units += [("w1", E - 1, 1), ("w2", E - 1, 0)]
         raws = {}
-        gates = {}
+
+        gate_sb = keep.tile([P, E * C], F32, name="gate_sb", align_bytes=64)
+        gates = [gate_sb[:, e * C : (e + 1) * C] for e in range(E)]
+
 
         def load(i):
             kind, a, b = units[i]
-            raw = stage.tile([P, 4 * H + TAIL], F32, name="raw", tag="raw")
+            raw = stage.tile([P, 4 * H], F32, name="raw", tag="raw")
             if kind == "x":
                 view = raw[:, : 2 * T].rearrange("p (e n) -> p e n", e=2)
                 nc.sync.dma_start(out=view, in_=x_view[a, b])
@@ -93,12 +88,6 @@ def tile_routed_moe_kernel(tc, xT, w1, w2, gate, offs, out):
                 view = raw[:, : 4 * N].rearrange("p (j n) -> p j n", j=4)
                 nc.sync.dma_start(out=view, in_=w2_view[a])
             raws[i] = view
-            slots = gate_slots(kind, a, b)
-            if slots is not None:
-                lo, hi = slots
-                nc.sync.dma_start(out=raw[:, 4 * H : 4 * H + (hi - lo) * C], in_=gate[0:P, lo * C : hi * C])
-                for e in range(lo, hi):
-                    gates[e] = raw[:, 4 * H + (e - lo) * C : 4 * H + (e - lo + 1) * C]
 
         w1c = {}
         w2c = {}
@@ -106,31 +95,44 @@ def tile_routed_moe_kernel(tc, xT, w1, w2, gate, offs, out):
 
         def do_x(i, g, u):
             raw = raws[i]
-            for s in range(2):
+            nx = len(X_ENGINE[(g, u)])
+            for q in range(nx):
+                cols = slice(q * T // nx, (q + 1) * T // nx)
                 cast(
                     nc,
-                    X_ENGINE[(g, u)][s],
-                    pairs[(g, u)][:, s * HALF : (s + 1) * HALF, :].rearrange("p (c i) e -> p c e i", i=4),
-                    raw[:, :, s * HALF : (s + 1) * HALF].rearrange("p e (c i) -> p c e i", i=4),
+                    X_ENGINE[(g, u)][q],
+                    pairs[(g, u)][:, cols, :].rearrange("p (c i) e -> p c e i", i=4),
+                    raw[:, :, cols].rearrange("p e (c i) -> p c e i", i=4),
                 )
             window = pairs[(g, u)][:].rearrange("p n e -> p (n e)").bitcast(U32)
-            words = xg[g][:].rearrange("p n t -> p (n t)").bitcast(U32).rearrange("p (n u) -> p n u", u=2)
+            apart = picked[g][:].rearrange("p u n e -> p (u n e)").bitcast(U32).rearrange("p (u n) -> p u n", u=2)
             for s in range(2):
                 nc.vector.tensor_copy(
-                    out=words[:, s * HALF : (s + 1) * HALF, u],
+                    out=apart[:, u, s * HALF : (s + 1) * HALF],
                     in_=window.indirect(offs_sb[:, s * (HALF // 16) : (s + 1) * (HALF // 16)]),
                 )
             if u == 1:
+                words = xg[g][:].rearrange("p n t -> p (n t)").bitcast(U32).rearrange("p (n u) -> p n u", u=2)
                 for s in range(2):
                     cols = slice(s * HALF, (s + 1) * HALF)
-                    nc.vector.quantize_mx(
-                        out=xc[g][:, cols].bitcast(FP8X4),
-                        scales=xs[g][:, cols],
-                        in_=xg[g][:, cols, :].rearrange("p n t -> p (n t)"),
-                    )
+                    nc.gpsimd.tensor_copy(out=words[:, cols, :], in_=apart[:, :, cols].rearrange("p u n -> p n u"))
+            if (g, u) == (PASSES - 1, 1):
+                for q in range(PASSES):
+                    tag = "pairs%d1" % (PASSES - 1) if q == 0 else "xc"
+                    xc.append(keep.tile([P, E * C], U32, name="xc%d" % q, tag=tag, align_bytes=64))
+                    for s in range(2):
+                        cols = slice(s * HALF, (s + 1) * HALF)
+                        nc.vector.quantize_mx(
+                            out=xc[q][:, cols].bitcast(FP8X4),
+                            scales=xs[q][:, cols],
+                            in_=xg[q][:, cols, :].rearrange("p n t -> p (n t)"),
+                        )
 
         def do_w1(i, e, g):
-            wg = grouped1.tile([P, 4 * H], BF16, name="wg", tag="wg", align_bytes=64)
+            if g == PASSES - 1:
+                wg = grouped1.tile([P, 4 * H], BF16, name="wg", tag="turn%d" % (e % 2), bufs=1, align_bytes=64)
+            else:
+                wg = grouped1.tile([P, 4 * H], BF16, name="wg", tag="wg", bufs=3, align_bytes=64)
             cast(
                 nc,
                 "S",
@@ -187,32 +189,41 @@ def tile_routed_moe_kernel(tc, xT, w1, w2, gate, offs, out):
                 )
             w2c[e] = (wc, ws)
 
-        def finish(e, b0, width, tag, bufs):
+        def finish(e, b0, steps, tag, bufs):
             hcod, hsc = hc[e]
             wc, ws = w2c[e]
             ocols = offs_sb[:, e * (C // 16) : (e + 1) * (C // 16)]
-            y_ps = psum_y.tile([P, width, C], F32, name="y_ps", tag="y_ps")
-            for r in range(width):
-                cols = slice((b0 + r) * P, (b0 + r + 1) * P)
-                nc.tensor.matmul_mx(
-                    out=y_ps[:, r, :],
-                    lhsT=wc[:, cols].bitcast(FP8X4),
-                    lhsT_scale=ws[:, cols],
-                    rhs=hcod[:].bitcast(FP8X4),
-                    rhs_scale=hsc[:],
-                    start=True,
-                    stop=True,
-                )
-            y_sb = small.tile([P, width, C], F32, name="y_sb", tag=tag, bufs=bufs, align_bytes=64)
-            if e < E - 1:
-                nc.vector.tensor_tensor(
-                    out=y_sb[:],
-                    in0=y_ps[:],
-                    in1=gates[e].unsqueeze(1).to_broadcast([P, width, C]),
-                    op=MULT,
+            width = sum(steps)
+            if tag == "turn":
+                y_sb = grouped1.tile(
+                    [P, width, C], F32, name="y_sb", tag="turn%d" % ((e + 1) % 2), bufs=1, align_bytes=64
                 )
             else:
-                nc.scalar.copy(out=y_sb[:], in_=y_ps[:])
+                y_sb = small.tile([P, width, C], F32, name="y_sb", tag=tag, bufs=bufs, align_bytes=64)
+            o = 0
+            for w in steps:
+                y_ps = psum_y.tile([P, w, C], F32, name="y_ps", tag="y_ps")
+                for r in range(w):
+                    cols = slice((b0 + o + r) * P, (b0 + o + r + 1) * P)
+                    nc.tensor.matmul_mx(
+                        out=y_ps[:, r, :],
+                        lhsT=wc[:, cols].bitcast(FP8X4),
+                        lhsT_scale=ws[:, cols],
+                        rhs=hcod[:].bitcast(FP8X4),
+                        rhs_scale=hsc[:],
+                        start=True,
+                        stop=True,
+                    )
+                if e < E - 1:
+                    nc.vector.tensor_tensor(
+                        out=y_sb[:, o : o + w, :],
+                        in0=y_ps[:],
+                        in1=gates[e].unsqueeze(1).to_broadcast([P, w, C]),
+                        op=MULT,
+                    )
+                else:
+                    nc.scalar.copy(out=y_sb[:, o : o + w, :], in_=y_ps[:])
+                o = o + w
             for r in range(width):
                 window = out_sb[b0 + r][:].indirect(ocols)
                 if e < E - 1:
@@ -224,17 +235,19 @@ def tile_routed_moe_kernel(tc, xT, w1, w2, gate, offs, out):
             nc.sync.dma_start(out=out[b * P : (b + 1) * P, :], in_=out_sb[b][:])
 
         def finish_last_two():
-            finish(E - 2, 0, 2, "y2", 4)
-            finish(E - 2, 2, 1, "tail_h", 1)
-            finish(E - 1, 0, 1, "tail_y", 1)
+            finish(E - 2, 0, (1, 1), "turn", 1)
+            finish(E - 2, 2, (1,), "tail_h", 1)
+            finish(E - 1, 0, (1,), "tail_y", 1)
             store(0)
-            finish(E - 2, 3, 1, "tail_y", 1)
+            finish(E - 2, 3, (1,), "tail_y", 1)
             for b in range(1, 4):
-                finish(E - 1, b, 1, "y1", 4)
+                finish(E - 1, b, (1,), "y", 4)
                 store(b)
 
         for i in range(min(STAGE_BUFS, len(units))):
             load(i)
+            if i == 2 * PASSES - 1:
+                nc.sync.dma_start(out=gate_sb[:], in_=gate[0:P, :])
         done = {"x": 0, "l1": 0, "l2": 0}
         for i in range(len(units)):
             kind, a, b = units[i]
@@ -251,11 +264,10 @@ def tile_routed_moe_kernel(tc, xT, w1, w2, gate, offs, out):
                 while done["l1"] < E and (done["l1"], PASSES - 1) in w1c:
                     layer1(done["l1"])
                     done["l1"] = done["l1"] + 1
-                while done["l2"] < done["l1"] and done["l2"] in w2c and done["l2"] in gates:
+                while done["l2"] < E and done["l2"] in w2c and done["l1"] > min(done["l2"] + 1, E - 1):
                     e = done["l2"]
                     if e < E - 2:
-                        finish(e, 0, 2, "y2", 4)
-                        finish(e, 2, 2, "y2", 4)
+                        finish(e, 0, (1, 3), "turn", 1)
                     elif e == E - 1:
                         finish_last_two()
                     done["l2"] = e + 1

@@ -22,6 +22,7 @@ HALF = 512
 
 X_ENGINE = {(0, 0): "VS", (0, 1): "S", (1, 0): "S", (1, 1): "S"}
 W2_ENGINE = ["GSGS"] * (E - 1) + ["SSSS"]
+W1_STEP = (4, 2)
 
 
 def cast(nc, engine, out, in_):
@@ -65,8 +66,8 @@ def tile_routed_moe_kernel(tc, xT, w1, w2, gate, offs, out):
         w2_view = w2.rearrange("e (p j) n -> e p j n", p=P, j=4)
 
         units = [("x", g, u) for g in range(PASSES) for u in range(2)]
-        units += [("w1", 0, 0), ("w1", 1, 0), ("w2", 0, 0), ("w1", 0, 1)]
-        for e in range(1, E - 1):
+        units += [("w1", 0, 0)]
+        for e in range(E - 1):
             units += [("w1", e, 1), ("w1", e + 1, 0), ("w2", e, 0)]
         units += [("w1", E - 1, 1), ("w2", E - 1, 0)]
         raws = {}
@@ -133,15 +134,20 @@ def tile_routed_moe_kernel(tc, xT, w1, w2, gate, offs, out):
                 wg = grouped1.tile([P, 4 * H], BF16, name="wg", tag="turn%d" % (e % 2), bufs=1, align_bytes=64)
             else:
                 wg = grouped1.tile([P, 4 * H], BF16, name="wg", tag="wg", bufs=3, align_bytes=64)
-            cast(
-                nc,
-                "S",
-                wg[:].rearrange("p (t m j) -> p m j t", t=4, m=P, j=4),
-                raws[i].rearrange("p j (m t) -> p m j t", t=4),
-            )
             wc = codes1.tile([P, H], U32, name="wc", tag="wc", align_bytes=64)
             ws = codes1.tile([P, H], U8, name="ws", tag="ws", align_bytes=64)
-            nc.vector.quantize_mx(out=wc[:].bitcast(FP8X4), scales=ws[:], in_=wg[:])
+            step = W1_STEP[g]
+            for t in range(0, 4, step):
+                cast(
+                    nc,
+                    "S",
+                    wg[:].rearrange("p (t m j) -> p m j t", t=4, m=P, j=4)[:, :, :, t : t + step],
+                    raws[i].rearrange("p j (m t) -> p m j t", t=4)[:, :, :, t : t + step],
+                )
+                cols = slice(t * P, (t + step) * P)
+                nc.vector.quantize_mx(
+                    out=wc[:, cols].bitcast(FP8X4), scales=ws[:, cols], in_=wg[:, t * 4 * P : (t + step) * 4 * P]
+                )
             w1c[(e, g)] = (wc, ws)
 
         def layer1(e):

@@ -20,8 +20,8 @@ PASSES = K // 512
 STAGE_BUFS = 10
 HALF = 512
 
-X_ENGINE = {(0, 0): "VS", (0, 1): "S", (1, 0): "S", (1, 1): "S"}
-W2_ENGINE = ["GSGS"] * (E - 1) + ["SSSS"]
+X_ENGINE = {(0, 0): "VV", (0, 1): "GV", (1, 0): "S", (1, 1): "S"}
+W2_ENGINE = ["VSVS"] + ["GSGS"] * (E - 2) + ["SSSS"]
 W1_STEP = (4, 2)
 
 
@@ -66,14 +66,28 @@ def tile_routed_moe_kernel(tc, xT, w1, w2, gate, offs, out):
         w2_view = w2.rearrange("e (p j) n -> e p j n", p=P, j=4)
 
         units = [("x", g, u) for g in range(PASSES) for u in range(2)]
-        units += [("w1", 0, 0)]
-        for e in range(E - 1):
+        units += [("w1", 0, 0), ("w1", 1, 0), ("w2", 0, 0), ("w1", 0, 1)]
+        for e in range(1, E - 1):
             units += [("w1", e, 1), ("w1", e + 1, 0), ("w2", e, 0)]
         units += [("w1", E - 1, 1), ("w2", E - 1, 0)]
         raws = {}
 
+        ones = lists.tile([P, P], F32, name="ones", align_bytes=64)
+        gate_row = lists.tile([P, E * C], F32, name="gate_row", align_bytes=64)
         gate_sb = keep.tile([P, E * C], F32, name="gate_sb", align_bytes=64)
         gates = [gate_sb[:, e * C : (e + 1) * C] for e in range(E)]
+
+        def load_gate():
+            nc.gpsimd.memset(gate_row[:], 0.0)
+            nc.gpsimd.memset(ones[:], 1.0)
+            row = lists.tile([1, E * C], F32, name="row")
+            nc.sync.dma_start(out=row[:], in_=gate[0:1, :])
+            nc.vector.tensor_copy(out=gate_row[0:1, :], in_=row[:])
+            for s in range(2):
+                cols = slice(s * HALF, (s + 1) * HALF)
+                g_ps = psum_a.tile([P, HALF], F32, name="g_ps", tag="a_ps")
+                nc.tensor.matmul(out=g_ps[:], lhsT=ones[:], rhs=gate_row[:, cols], start=True, stop=True)
+                nc.scalar.copy(out=gate_sb[:, cols], in_=g_ps[:])
 
 
         def load(i):
@@ -187,7 +201,7 @@ def tile_routed_moe_kernel(tc, xT, w1, w2, gate, offs, out):
                     wg[:, b * 4 * P : (b + 1) * 4 * P].rearrange("p (c i j) -> p c j i", i=4, j=4),
                     raw[:, :, b * P : (b + 1) * P].rearrange("p j (c i) -> p c j i", i=4),
                 )
-            step = 4 if e < E - 1 else 1
+            step = 4 if e < E - 1 else 2
             for b in range(0, 4, step):
                 cols = slice(b * P, (b + step) * P)
                 nc.vector.quantize_mx(
@@ -250,10 +264,9 @@ def tile_routed_moe_kernel(tc, xT, w1, w2, gate, offs, out):
                 finish(E - 1, b, (1,), "y", 4)
                 store(b)
 
+        load_gate()
         for i in range(min(STAGE_BUFS, len(units))):
             load(i)
-            if i == 2 * PASSES - 1:
-                nc.sync.dma_start(out=gate_sb[:], in_=gate[0:P, :])
         done = {"x": 0, "l1": 0, "l2": 0}
         for i in range(len(units)):
             kind, a, b = units[i]

@@ -21,7 +21,10 @@ STAGE_BUFS = 10
 HALF = 512
 
 X_ENGINE = {(0, 0): "VV", (0, 1): "GV", (1, 0): "S", (1, 1): "S"}
-W2_ENGINE = ["VSVS"] + ["GSGS"] * (E - 2) + ["SSSS"]
+W1_SHARES = ((("S", 0, P),), (("S", 0, P),))
+W2_FIRST = (("V", 0, 2), ("S", 2, 4))
+W2_SHARES = (("G", 0, 2), ("S", 2, 4))
+W2_LAST = (("S", 0, 2), ("S", 2, 4))
 W1_STEP = (4, 2)
 
 
@@ -152,12 +155,13 @@ def tile_routed_moe_kernel(tc, xT, w1, w2, gate, offs, out):
             ws = codes1.tile([P, H], U8, name="ws", tag="ws", align_bytes=64)
             step = W1_STEP[g]
             for t in range(0, 4, step):
-                cast(
-                    nc,
-                    "S",
-                    wg[:].rearrange("p (t m j) -> p m j t", t=4, m=P, j=4)[:, :, :, t : t + step],
-                    raws[i].rearrange("p j (m t) -> p m j t", t=4)[:, :, :, t : t + step],
-                )
+                for engine, lo, hi in W1_SHARES[g]:
+                    cast(
+                        nc,
+                        engine,
+                        wg[:].rearrange("p (t m j) -> p m j t", t=4, m=P, j=4)[:, lo:hi, :, t : t + step],
+                        raws[i].rearrange("p j (m t) -> p m j t", t=4)[:, lo:hi, :, t : t + step],
+                    )
                 cols = slice(t * P, (t + step) * P)
                 nc.vector.quantize_mx(
                     out=wc[:, cols].bitcast(FP8X4), scales=ws[:, cols], in_=wg[:, t * 4 * P : (t + step) * 4 * P]
@@ -194,12 +198,12 @@ def tile_routed_moe_kernel(tc, xT, w1, w2, gate, offs, out):
             wg = grouped2.tile([P, 4 * N], BF16, name="wg", tag="wg", align_bytes=64)
             wc = codes2.tile([P, N], U32, name="wc", tag="wc", align_bytes=64)
             ws = codes2.tile([P, N], U8, name="ws", tag="ws", align_bytes=64)
-            for b in range(4):
+            for engine, lo, hi in W2_FIRST if e == 0 else W2_LAST if e == E - 1 else W2_SHARES:
                 cast(
                     nc,
-                    W2_ENGINE[e][b],
-                    wg[:, b * 4 * P : (b + 1) * 4 * P].rearrange("p (c i j) -> p c j i", i=4, j=4),
-                    raw[:, :, b * P : (b + 1) * P].rearrange("p j (c i) -> p c j i", i=4),
+                    engine,
+                    wg[:, lo * 4 * P : hi * 4 * P].rearrange("p (c i j) -> p c j i", i=4, j=4),
+                    raw[:, :, lo * P : hi * P].rearrange("p j (c i) -> p c j i", i=4),
                 )
             step = 4 if e < E - 1 else 2
             for b in range(0, 4, step):

from contextlib import ExitStack

import concourse.mybir as mybir

K, T, E, C, H, N = 1024, 1024, 8, 128, 512, 512
FLOPS = 2 * E * C * (K * H + H * N)

F32 = mybir.dt.float32
BF16 = mybir.dt.bfloat16
U32 = mybir.dt.uint32
U16 = mybir.dt.uint16
U8 = mybir.dt.uint8
FP8X4 = mybir.dt.float8_e4m3fn_x4
MULT = mybir.AluOpType.mult
ADD = mybir.AluOpType.add
RELU = mybir.ActivationFunctionType.Relu

P = 128
PASSES = K // 512
STAGE_BUFS = 10
HALF = 512

X_ENGINE = {(0, 0): "VV", (0, 1): "GV", (1, 0): "S", (1, 1): "S"}
W1_SHARES = ((("S", 0, P),), (("S", 0, P),))
W2_FIRST = (("V", 0, 2), ("S", 2, 4))
W2_SHARES = (("G", 0, 2), ("S", 2, 4))
W2_LAST = (("S", 0, 2), ("S", 2, 4))
W1_STEP = (4, 2)


def cast(nc, engine, out, in_):
    if engine == "V":
        nc.vector.tensor_copy(out=out, in_=in_)
    elif engine == "S":
        nc.scalar.copy(out=out, in_=in_)
    else:
        nc.gpsimd.tensor_scalar(out, in_, 1.0, 0.0, op0=MULT, op1=ADD)


def tile_routed_moe_kernel(tc, xT, w1, w2, gate, offs, out):
    nc = tc.nc
    with ExitStack() as ctx:
        lists = ctx.enter_context(tc.tile_pool(name="lists", bufs=1))
        keep = ctx.enter_context(tc.tile_pool(name="keep", bufs=1))
        stage = ctx.enter_context(tc.tile_pool(name="stage", bufs=STAGE_BUFS))
        grouped1 = ctx.enter_context(tc.tile_pool(name="grouped1", bufs=4))
        grouped2 = ctx.enter_context(tc.tile_pool(name="grouped2", bufs=3))
        codes1 = ctx.enter_context(tc.tile_pool(name="codes1", bufs=8))
        codes2 = ctx.enter_context(tc.tile_pool(name="codes2", bufs=4))
        small = ctx.enter_context(tc.tile_pool(name="small", bufs=3))
        psum_a = ctx.enter_context(tc.psum_pool(name="psum_a", bufs=3))
        psum_y = ctx.enter_context(tc.psum_pool(name="psum_y", bufs=4))

        offs_sb = lists.tile([P, E * C // 16], U16, name="offs_sb")
        nc.sync.dma_start(offs_sb[:], offs)

        pairs = {}
        for g in range(PASSES):
            for u in range(2):
                pairs[(g, u)] = keep.tile([P, T, 2], BF16, name="pairs%d%d" % (g, u), tag="pairs%d%d" % (g, u), align_bytes=64)
        xg = [keep.tile([P, E * C, 4], BF16, name="xg%d" % g, align_bytes=64) for g in range(PASSES)]
        picked = [keep.tile([P, 2, E * C, 2], BF16, name="picked%d" % g, align_bytes=64) for g in range(PASSES)]
        xc = []
        xs = [keep.tile([P, E * C], U8, name="xs%d" % g, align_bytes=64) for g in range(PASSES)]
        out_sb = [keep.tile([P, T], F32, name="out_sb%d" % b) for b in range(4)]

        x_view = xT.rearrange("(g p u e) n -> g u p e n", g=PASSES, p=P, u=2, e=2)
        w1_view = w1.rearrange("e (g p j) i -> e g p j i", g=PASSES, p=P, j=4)
        w2_view = w2.rearrange("e (p j) n -> e p j n", p=P, j=4)

        units = [("x", g, u) for g in range(PASSES) for u in range(2)]
        units += [("w1", 0, 0), ("w1", 1, 0), ("w2", 0, 0), ("w1", 0, 1)]
        for e in range(1, E - 1):
            units += [("w1", e, 1), ("w1", e + 1, 0), ("w2", e, 0)]
        units += [("w1", E - 1, 1), ("w2", E - 1, 0)]
        raws = {}

        ones = lists.tile([P, P], F32, name="ones", align_bytes=64)
        gate_row = lists.tile([P, E * C], F32, name="gate_row", align_bytes=64)
        gate_sb = keep.tile([P, E * C], F32, name="gate_sb", align_bytes=64)
        gates = [gate_sb[:, e * C : (e + 1) * C] for e in range(E)]

        def load_gate():
            nc.gpsimd.memset(gate_row[:], 0.0)
            nc.gpsimd.memset(ones[:], 1.0)
            row = lists.tile([1, E * C], F32, name="row")
            nc.sync.dma_start(out=row[:], in_=gate[0:1, :])
            nc.vector.tensor_copy(out=gate_row[0:1, :], in_=row[:])
            for s in range(2):
                cols = slice(s * HALF, (s + 1) * HALF)
                g_ps = psum_a.tile([P, HALF], F32, name="g_ps", tag="a_ps")
                nc.tensor.matmul(out=g_ps[:], lhsT=ones[:], rhs=gate_row[:, cols], start=True, stop=True)
                nc.scalar.copy(out=gate_sb[:, cols], in_=g_ps[:])


        def load(i):
            kind, a, b = units[i]
            raw = stage.tile([P, 4 * H], F32, name="raw", tag="raw")
            if kind == "x":
                view = raw[:, : 2 * T].rearrange("p (e n) -> p e n", e=2)
                nc.sync.dma_start(out=view, in_=x_view[a, b])
            elif kind == "w1":
                view = raw[:, : 4 * H].rearrange("p (j i) -> p j i", j=4)
                nc.sync.dma_start(out=view, in_=w1_view[a, b])
            else:
                view = raw[:, : 4 * N].rearrange("p (j n) -> p j n", j=4)
                nc.sync.dma_start(out=view, in_=w2_view[a])
            raws[i] = view

        w1c = {}
        w2c = {}
        hc = {}

        def do_x(i, g, u):
            raw = raws[i]
            nx = len(X_ENGINE[(g, u)])
            for q in range(nx):
                cols = slice(q * T // nx, (q + 1) * T // nx)
                cast(
                    nc,
                    X_ENGINE[(g, u)][q],
                    pairs[(g, u)][:, cols, :].rearrange("p (c i) e -> p c e i", i=4),
                    raw[:, :, cols].rearrange("p e (c i) -> p c e i", i=4),
                )
            window = pairs[(g, u)][:].rearrange("p n e -> p (n e)").bitcast(U32)
            apart = picked[g][:].rearrange("p u n e -> p (u n e)").bitcast(U32).rearrange("p (u n) -> p u n", u=2)
            for s in range(2):
                nc.vector.tensor_copy(
                    out=apart[:, u, s * HALF : (s + 1) * HALF],
                    in_=window.indirect(offs_sb[:, s * (HALF // 16) : (s + 1) * (HALF // 16)]),
                )
            if u == 1:
                words = xg[g][:].rearrange("p n t -> p (n t)").bitcast(U32).rearrange("p (n u) -> p n u", u=2)
                for s in range(2):
                    cols = slice(s * HALF, (s + 1) * HALF)
                    nc.gpsimd.tensor_copy(out=words[:, cols, :], in_=apart[:, :, cols].rearrange("p u n -> p n u"))
            if (g, u) == (PASSES - 1, 1):
                for q in range(PASSES):
                    tag = "pairs%d1" % (PASSES - 1) if q == 0 else "xc"
                    xc.append(keep.tile([P, E * C], U32, name="xc%d" % q, tag=tag, align_bytes=64))
                    for s in range(2):
                        cols = slice(s * HALF, (s + 1) * HALF)
                        nc.vector.quantize_mx(
                            out=xc[q][:, cols].bitcast(FP8X4),
                            scales=xs[q][:, cols],
                            in_=xg[q][:, cols, :].rearrange("p n t -> p (n t)"),
                        )

        def do_w1(i, e, g):
            if g == PASSES - 1:
                wg = grouped1.tile([P, 4 * H], BF16, name="wg", tag="turn%d" % (e % 2), bufs=1, align_bytes=64)
            else:
                wg = grouped1.tile([P, 4 * H], BF16, name="wg", tag="wg", bufs=3, align_bytes=64)
            wc = codes1.tile([P, H], U32, name="wc", tag="wc", align_bytes=64)
            ws = codes1.tile([P, H], U8, name="ws", tag="ws", align_bytes=64)
            step = W1_STEP[g]
            for t in range(0, 4, step):
                for engine, lo, hi in W1_SHARES[g]:
                    cast(
                        nc,
                        engine,
                        wg[:].rearrange("p (t m j) -> p m j t", t=4, m=P, j=4)[:, lo:hi, :, t : t + step],
                        raws[i].rearrange("p j (m t) -> p m j t", t=4)[:, lo:hi, :, t : t + step],
                    )
                cols = slice(t * P, (t + step) * P)
                nc.vector.quantize_mx(
                    out=wc[:, cols].bitcast(FP8X4), scales=ws[:, cols], in_=wg[:, t * 4 * P : (t + step) * 4 * P]
                )
            w1c[(e, g)] = (wc, ws)

        def layer1(e):
            a_ps = psum_a.tile([P, 4, C], F32, name="a_ps", tag="a_ps")
            slots = slice(e * C, (e + 1) * C)
            for t in range(4):
                for g in range(PASSES):
                    wc, ws = w1c[(e, g)]
                    nc.tensor.matmul_mx(
                        out=a_ps[:, t, :],
                        lhsT=wc[:, t * P : (t + 1) * P].bitcast(FP8X4),
                        lhsT_scale=ws[:, t * P : (t + 1) * P],
                        rhs=xc[g][:, slots].bitcast(FP8X4),
                        rhs_scale=xs[g][:, slots],
                        start=(g == 0),
                        stop=(g == PASSES - 1),
                    )
            if e == E - 1:
                hb = small.tile([P, C, 4], BF16, name="hb", tag="tail_h", bufs=1, align_bytes=64)
            else:
                hb = small.tile([P, C, 4], BF16, name="hb", tag="hb", align_bytes=64)
            nc.scalar.activation(out=hb[:], in_=a_ps[:].rearrange("p t n -> p n t"), func=RELU)
            hcod = small.tile([P, C], U32, name="hcod", tag="hcod", align_bytes=64)
            hsc = small.tile([P, C], U8, name="hsc", tag="hsc", align_bytes=64)
            nc.vector.quantize_mx(out=hcod[:].bitcast(FP8X4), scales=hsc[:], in_=hb[:].rearrange("p n t -> p (n t)"))
            hc[e] = (hcod, hsc)

        def do_w2(i, e):
            raw = raws[i]
            wg = grouped2.tile([P, 4 * N], BF16, name="wg", tag="wg", align_bytes=64)
            wc = codes2.tile([P, N], U32, name="wc", tag="wc", align_bytes=64)
            ws = codes2.tile([P, N], U8, name="ws", tag="ws", align_bytes=64)
            for engine, lo, hi in W2_FIRST if e == 0 else W2_LAST if e == E - 1 else W2_SHARES:
                cast(
                    nc,
                    engine,
                    wg[:, lo * 4 * P : hi * 4 * P].rearrange("p (c i j) -> p c j i", i=4, j=4),
                    raw[:, :, lo * P : hi * P].rearrange("p j (c i) -> p c j i", i=4),
                )
            step = 4 if e < E - 1 else 2
            for b in range(0, 4, step):
                cols = slice(b * P, (b + step) * P)
                nc.vector.quantize_mx(
                    out=wc[:, cols].bitcast(FP8X4), scales=ws[:, cols], in_=wg[:, b * 4 * P : (b + step) * 4 * P]
                )
            w2c[e] = (wc, ws)

        def finish(e, b0, steps, tag, bufs):
            hcod, hsc = hc[e]
            wc, ws = w2c[e]
            ocols = offs_sb[:, e * (C // 16) : (e + 1) * (C // 16)]
            width = sum(steps)
            if tag == "turn":
                y_sb = grouped1.tile(
                    [P, width, C], F32, name="y_sb", tag="turn%d" % ((e + 1) % 2), bufs=1, align_bytes=64
                )
            else:
                y_sb = small.tile([P, width, C], F32, name="y_sb", tag=tag, bufs=bufs, align_bytes=64)
            o = 0
            for w in steps:
                y_ps = psum_y.tile([P, w, C], F32, name="y_ps", tag="y_ps")
                for r in range(w):
                    cols = slice((b0 + o + r) * P, (b0 + o + r + 1) * P)
                    nc.tensor.matmul_mx(
                        out=y_ps[:, r, :],
                        lhsT=wc[:, cols].bitcast(FP8X4),
                        lhsT_scale=ws[:, cols],
                        rhs=hcod[:].bitcast(FP8X4),
                        rhs_scale=hsc[:],
                        start=True,
                        stop=True,
                    )
                if e < E - 1:
                    nc.vector.tensor_tensor(
                        out=y_sb[:, o : o + w, :],
                        in0=y_ps[:],
                        in1=gates[e].unsqueeze(1).to_broadcast([P, w, C]),
                        op=MULT,
                    )
                else:
                    nc.scalar.copy(out=y_sb[:, o : o + w, :], in_=y_ps[:])
                o = o + w
            for r in range(width):
                window = out_sb[b0 + r][:].indirect(ocols)
                if e < E - 1:
                    nc.vector.tensor_copy(out=window, in_=y_sb[:, r, :])
                else:
                    nc.vector.tensor_tensor(out=window, in0=y_sb[:, r, :], in1=gates[e], op=MULT)

        def store(b):
            nc.sync.dma_start(out=out[b * P : (b + 1) * P, :], in_=out_sb[b][:])

        def finish_last_two():
            finish(E - 2, 0, (1, 1), "turn", 1)
            finish(E - 2, 2, (1,), "tail_h", 1)
            finish(E - 1, 0, (1,), "tail_y", 1)
            store(0)
            finish(E - 2, 3, (1,), "tail_y", 1)
            for b in range(1, 4):
                finish(E - 1, b, (1,), "y", 4)
                store(b)

        load_gate()
        for i in range(min(STAGE_BUFS, len(units))):
            load(i)
        done = {"x": 0, "l1": 0, "l2": 0}
        for i in range(len(units)):
            kind, a, b = units[i]
            if kind == "x":
                do_x(i, a, b)
                done["x"] = done["x"] + 1
            elif kind == "w1":
                do_w1(i, a, b)
            else:
                do_w2(i, a)
            if i + STAGE_BUFS < len(units):
                load(i + STAGE_BUFS)
            if done["x"] == 2 * PASSES:
                while done["l1"] < E and (done["l1"], PASSES - 1) in w1c:
                    layer1(done["l1"])
                    done["l1"] = done["l1"] + 1
                while done["l2"] < E and done["l2"] in w2c and done["l1"] > min(done["l2"] + 1, E - 1):
                    e = done["l2"]
                    if e < E - 2:
                        finish(e, 0, (1, 3), "turn", 1)
                    elif e == E - 1:
                        finish_last_two()
                    done["l2"] = e + 1
